import numpy as np
import ml_dtypes


def mxq(x, axis, fmt="e4m3"):
    dtype, down = {"e4m3": (ml_dtypes.float8_e4m3fn, 7), "e5m2": (ml_dtypes.float8_e5m2, 14)}[fmt]
    v = np.moveaxis(np.asarray(x, np.float32).astype(ml_dtypes.bfloat16).astype(np.float64), axis, -1)
    blocks = v.reshape(v.shape[:-1] + (-1, 32))
    amax = np.abs(blocks).max(-1, keepdims=True)
    byte = np.maximum(np.where(amax > 0, np.frexp(amax)[1] - 1 + 127, 0) - down, 1)
    scale = np.exp2(byte - 127.0)
    codes = (blocks / scale).astype(np.float32).astype(dtype).astype(np.float64)
    return np.moveaxis((codes * scale).reshape(v.shape), -1, axis)


WIDE = False


def mx_kscale(k):
    if not WIDE:
        return np.ones(k)
    levels = np.array([10, -10, 5, -5, 0])
    if k % 512:
        return np.exp2(np.random.permutation(np.resize(levels, k // 32))).repeat(32)
    a = np.empty((k // 512, 16))
    for p in range(k // 512):
        a[p, :8] = np.random.permutation(np.resize(levels, 8))
        for g in range(8):
            far = levels[np.abs(levels - a[p, g]) >= 10]
            a[p, g + 8] = far[np.random.randint(len(far))]
    return np.exp2(a.ravel()).repeat(32)


def f64(x):
    return np.asarray(x).astype(np.float64)


def striped(idx):
    return np.tile(np.asarray(idx).reshape(-1, 16).T, (8, 1)).astype(np.uint16)


def unstriped(offs):
    return offs[:16].T.reshape(-1).astype(np.int64)


E2M1 = np.array([0.0, 0.5, 1.0, 1.5, 2.0, 3.0, 4.0, 6.0, -0.0, -0.5, -1.0, -1.5, -2.0, -3.0, -4.0, -6.0])


def pack_weight(w, fmt):
    k, n = w.shape
    w = f64(np.asarray(w, np.float32).astype(ml_dtypes.bfloat16)).reshape(k // 32, 32, n)
    amax = np.abs(w).max(1)
    if fmt == "e4m3":
        byte = np.frexp(amax)[1] - 1 + 127 - 7
    else:
        mant, ex = np.frexp(amax / 6.0)
        byte = np.where(mant > 0.5, ex, ex - 1) + 127
    byte = np.clip(np.where(amax > 0, byte, 1), 1, 254)
    scaled = (w * np.exp2(127.0 - byte)[:, None, :]).reshape(k, n).astype(np.float32)
    by_word = np.ascontiguousarray(scaled.reshape(k // 512, 128, 4, n).transpose(0, 1, 3, 2))
    if fmt == "e4m3":
        words = by_word.astype(ml_dtypes.float8_e4m3fn).view(np.uint8)
    else:
        c = by_word.astype(ml_dtypes.float4_e2m1fn).view(np.uint8) & 0xF
        words = (c[..., 0::2] | (c[..., 1::2] << 4)).reshape(k // 512, 128, 2 * n)
    return np.ascontiguousarray(words), np.ascontiguousarray(byte.astype(np.uint8).reshape(k // 512, 16, n))


def unpack_weight(words, scales, fmt):
    g, _, n = scales.shape
    words = np.ascontiguousarray(words).reshape(g, 128, n, -1)
    if fmt == "e4m3":
        vals = words.view(ml_dtypes.float8_e4m3fn).astype(np.float64)
    else:
        nib = np.empty((g, 128, n, 4), np.uint8)
        nib[..., 0::2] = words & 0xF
        nib[..., 1::2] = words >> 4
        vals = E2M1[nib]
    vals = vals * np.repeat(np.exp2(scales.astype(np.float64) - 127.0), 8, axis=1)[..., None]
    return vals.transpose(0, 1, 3, 2).reshape(g * 512, n)


K, T, J, I, S, R, N = 1024, 2048, 1024, 512, 1024, 512, 512


def setup_inputs():
    n = np.random.standard_normal
    idx = np.random.permutation(T)[:J]
    idx2 = np.random.permutation(J)[:I]
    idx3 = np.random.permutation(S)[:I]
    fk = mx_kscale(K)
    fr = mx_kscale(R)
    xtp = pack_weight(n((K, T)) / fk[:, None], "e4m3")
    wap = pack_weight(n((K, R)) * 1 / np.sqrt(K) * fk[:, None] * fr, "e2m1")
    wbp = pack_weight(n((R, N)) * 1 / np.sqrt(R) / fr[:, None], "e4m3")
    return {
        "xt_words": xtp[0],
        "xt_scales": xtp[1],
        "wa_words": wap[0],
        "wa_scales": wap[1],
        "wb_words": wbp[0],
        "wb_scales": wbp[1],
        "old": (1.0 * n((N, S))).astype(np.float32),
        "offs": striped(idx),
        "offs2": striped(idx2),
        "offs3": striped(idx3),
    }


def reference(xt_words, xt_scales, wa_words, wa_scales, wb_words, wb_scales, old, offs, offs2, offs3):
    idx = unstriped(offs)
    idx2 = unstriped(offs2)
    idx3 = unstriped(offs3)
    xtu = unpack_weight(xt_words, xt_scales, "e4m3")
    wau = unpack_weight(wa_words, wa_scales, "e2m1")
    wbu = unpack_weight(wb_words, wb_scales, "e4m3")
    xtidxg = xtu[:, idx]
    a = wau.T @ xtidxg
    hid = np.maximum(a, 0.0)
    hididx2q = mxq(hid[:, idx2], 0, "e4m3")
    p = wbu.T @ hididx2q
    pp = np.zeros((N, S))
    pp[:, idx3] = p
    y = pp + 0.3 * f64(old)
    return y

@@ -1,0 +1,274 @@
+from contextlib import ExitStack
+
+import concourse.mybir as mybir
+from concourse.masks import make_identity
+
+K, T, J, I, S, R, N = 1024, 2048, 1024, 512, 1024, 512, 512
+FLOPS = 2 * K * R * J + 2 * R * N * I
+
+F32 = mybir.dt.float32
+BF16 = mybir.dt.bfloat16
+I32 = mybir.dt.int32
+U32 = mybir.dt.uint32
+U16 = mybir.dt.uint16
+U8 = mybir.dt.uint8
+FP8X4 = mybir.dt.float8_e4m3fn_x4
+FP4X4 = mybir.dt.float4_e2m1fn_x4
+ACT = mybir.ActivationFunctionType
+ALU = mybir.AluOpType
+
+P = 128
+BANK = 512
+OLD_WEIGHT = 0.3
+
+
+def tile_moe_expert_relay_scattered_kernel(
+    tc, xt_words, xt_scales, wa_words, wa_scales, wb_words, wb_scales, old, offs, offs2, offs3, out
+):
+    nc = tc.nc
+    with ExitStack() as ctx:
+        lists = ctx.enter_context(tc.tile_pool(name="lists", bufs=1))
+        sb = ctx.enter_context(tc.tile_pool(name="sb", bufs=1))
+        late = ctx.enter_context(tc.tile_pool(name="late", bufs=1))
+        psum = ctx.enter_context(tc.psum_pool(name="psum", bufs=1))
+
+        def bank(b):
+            return psum.tile([P, BANK], F32, name="bank%d" % b, tag="bank%d" % b)
+
+        def entries(tile, first, count):
+            return tile[:, first // 16 : (first + count) // 16]
+
+        wa_planes_raw = sb.tile([P, 2 * R], U8, align_bytes=64)
+        nc.vector.memset(wa_planes_raw[:].bitcast(I32), 0)
+        x_rows = sb.tile([P, T], U8, align_bytes=64)
+        nc.vector.memset(x_rows[0:96, :].bitcast(I32), 0)
+        nc.sync.dma_start(x_rows[96:128, :].bitcast(I32), xt_scales.rearrange("z q c -> (z q) c").bitcast(I32))
+        idx = lists.tile([P, J // 16], U16)
+        nc.sync.dma_start(idx[:], offs)
+        wa_raw = sb.tile([P, 2, 2 * R], U8, tag="wb", align_bytes=64)
+        nc.sync.dma_start(wa_raw[:].bitcast(I32), wa_words.rearrange("z p c -> p z c").bitcast(I32))
+        x_win = [
+            sb.tile([P, T], I32, name="x_win0", tag="old_a", align_bytes=64),
+            late.tile([P, T], I32, name="x_win1", offset=0),
+        ]
+        nc.sync.dma_start(x_win[0][:], xt_words[0].rearrange("p c r -> p (c r)").bitcast(I32))
+        idx2 = lists.tile([P, I // 16], U16)
+        nc.sync.dma_start(idx2[:], offs2)
+        idx3 = lists.tile([P, I // 16], U16)
+        nc.sync.dma_start(idx3[:], offs3)
+        for q in range(4):
+            nc.sync.dma_start(
+                wa_planes_raw[32 * q : 32 * q + 4, :].bitcast(I32).rearrange("p (z c) -> p z c", z=2),
+                wa_scales[:, 4 * q : 4 * q + 4, :].rearrange("z q c -> q z c").bitcast(I32),
+            )
+        nc.sync.dma_start(x_win[1][:], xt_words[1].rearrange("p c r -> p (c r)").bitcast(I32))
+
+        xg_plane = [sb.tile([P, J], U8, name="xg_plane%d" % z, align_bytes=64) for z in range(2)]
+        for z in range(2):
+            nc.gpsimd.memset(xg_plane[z][:].bitcast(I32), 0)
+        places = [sb.tile([P, S], F32, name="places%d" % n) for n in range(2)]
+        for n in range(2):
+            nc.gpsimd.memset(places[n][:], 0.0)
+        ident = sb.tile([P, P], F32)
+        make_identity(nc, ident[:])
+        wb_planes = sb.tile([P, N], U8, align_bytes=64)
+        nc.gpsimd.memset(wb_planes[:].bitcast(I32), 0)
+
+        xg_rows = sb.tile([P, J], U8, align_bytes=64)
+        nc.vector.tensor_copy(xg_rows[:], x_rows[:].indirect(idx[:]))
+        for z in range(2):
+            for q in range(4):
+                first = 96 + 16 * z + 4 * q
+                nc.scalar.dma_start(
+                    xg_plane[z][32 * q : 32 * q + 4, :].bitcast(I32), xg_rows[first : first + 4, :].bitcast(I32)
+                )
+
+        for q in range(4):
+            nc.sync.dma_start(
+                wb_planes[32 * q : 32 * q + 4, :].bitcast(I32), wb_scales[0, 4 * q : 4 * q + 4, :].bitcast(I32)
+            )
+
+        wa_codes = sb.tile([P, 2, 2 * R], U8, align_bytes=64)
+        nc.vector.tensor_copy(
+            wa_codes[:].bitcast(U16).rearrange("p z (t b i) -> p z b t i", t=4, i=8),
+            wa_raw[:].bitcast(U16).rearrange("p z (b i t) -> p z b t i", t=4, i=8),
+        )
+        wa_planes = sb.tile([P, 2 * R], U8, align_bytes=64)
+        nc.vector.tensor_copy(
+            wa_planes[:].rearrange("p (z t b i) -> p z b t i", z=2, t=4, i=16),
+            wa_planes_raw[:].rearrange("p (z b i t) -> p z b t i", z=2, t=4, i=16),
+        )
+
+        wb_codes = sb.tile([P, N], I32, tag="wb", align_bytes=64)
+        nc.sync.dma_start(wb_codes[:], wb_words[0].rearrange("p c r -> p (c r)").bitcast(I32))
+
+        xg = [[sb.tile([P, BANK], U32, name="xg%d%d" % (z, h), tag="old_b" if z + h == 0 else "xg%d%d" % (z, h), align_bytes=64) for h in range(2)] for z in range(2)]
+        acc = {}
+
+        def first_product(t, z, h):
+            nc.tensor.matmul_mx(
+                out=acc[t, h][:],
+                lhsT=wa_codes[:, z, 256 * t : 256 * (t + 1)].bitcast(FP4X4),
+                lhsT_scale=wa_planes[:, R * z + P * t : R * z + P * (t + 1)],
+                rhs=xg[z][h][:].bitcast(FP8X4),
+                rhs_scale=xg_plane[z][:, BANK * h : BANK * (h + 1)],
+                start=(z == 0),
+                stop=(z == 1),
+            )
+
+        for z in range(2):
+            for h in range(2):
+                nc.vector.tensor_copy(xg[z][h][:], x_win[z][:].bitcast(U32).indirect(entries(idx, BANK * h, BANK)))
+        for h in range(2):
+            for t in range(2):
+                acc[t, h] = bank(2 * t + h)
+                first_product(t, 0, h)
+
+        old_sb = [sb.tile([P, 2, S], F32, name="old_" + c, tag="old_" + c, align_bytes=64) for c in "ab"]
+        for c in range(2):
+            nc.sync.dma_start(old_sb[c][:], old[256 * c : 256 * (c + 1), :].rearrange("(n p) s -> p n s", n=2))
+
+        for n in (2, 3):
+            places.append(late.tile([P, S], F32, name="places%d" % n, offset=4 * S * (n - 2)))
+            nc.vector.memset(places[n][:], 0.0)
+
+        hid = [sb.tile([P, J], F32, name="hid%d" % t) for t in range(4)]
+        for t in range(4):
+            for h in range(2):
+                if t >= 2:
+                    acc[t, h] = bank(2 * (t - 2) + h)
+                    first_product(t, 0, h)
+                first_product(t, 1, h)
+                nc.scalar.activation(hid[t][:, BANK * h : BANK * (h + 1)], acc[t, h][:], ACT.Relu)
+
+        picked = sb.tile([P, 4 * I], F32)
+        for t in range(3):
+            nc.vector.tensor_copy(picked[:, I * t : I * (t + 1)], hid[t][:].indirect(idx2[:]))
+        grouped = sb.tile([P, 4 * I], BF16, align_bytes=64)
+        h_codes = sb.tile([P, I], U32, align_bytes=64)
+        h_plane = sb.tile([P, I], U8, align_bytes=64)
+
+        def gather_last(first, count):
+            nc.vector.tensor_copy(
+                picked[:, 3 * I + first : 3 * I + first + count], hid[3][:].indirect(entries(idx2, first, count))
+            )
+
+        def interleave(first, count):
+            nc.scalar.copy(
+                grouped[:, 4 * first : 4 * (first + count)].rearrange("p (c i t) -> p c t i", i=4, t=4),
+                picked[:].rearrange("p (t c) -> p t c", t=4)[:, :, first : first + count].rearrange(
+                    "p t (c i) -> p c t i", i=4
+                ),
+            )
+
+        def quantise(first, count):
+            nc.vector.quantize_mx(
+                out=h_codes[:, first : first + count].bitcast(FP8X4),
+                scales=h_plane[:, first : first + count],
+                in_=grouped[:, 4 * first : 4 * (first + count)],
+            )
+
+        def second_product(dst, n, first, count):
+            nc.tensor.matmul_mx(
+                out=dst,
+                lhsT=wb_codes[:, P * n : P * (n + 1)].bitcast(FP8X4),
+                lhsT_scale=wb_planes[:, P * n : P * (n + 1)],
+                rhs=h_codes[:, first : first + count].bitcast(FP8X4),
+                rhs_scale=h_plane[:, first : first + count],
+                start=True,
+                stop=True,
+            )
+
+        def leave(dst, src, n):
+            nc.scalar.activation(dst, src, ACT.Copy, scale=1.0 / OLD_WEIGHT if n < 3 else 1.0)
+
+        def scatter(n, first, count, src):
+            nc.vector.tensor_copy(places[n][:].indirect(entries(idx3, first, count)), src)
+
+        gather_last(0, 128)
+        interleave(0, 128)
+        gather_last(128, 384)
+        quantise(0, 128)
+        interleave(128, 128)
+        head_bank = bank(4)
+        p_head = [sb.tile([P, P], F32, name="p_head%d" % n) for n in range(3)]
+        for n in range(3):
+            second_product(head_bank[:, P * n : P * (n + 1)], n, 0, 128)
+        for n in range(2):
+            leave(p_head[n][:], head_bank[:, P * n : P * (n + 1)], n)
+        quantise(128, 128)
+        interleave(256, 256)
+        leave(p_head[2][:], head_bank[:, 2 * P : 3 * P], 2)
+        b0_bank = bank(5)
+        second_product(b0_bank[:, 0:128], 0, 128, 128)
+        p_b0 = sb.tile([P, 128], F32)
+        leave(p_b0[:], b0_bank[:, 0:128], 0)
+        scatter(0, 0, 128, p_head[0][:])
+        scatter(1, 0, 128, p_head[1][:])
+        quantise(256, 256)
+        scatter(0, 128, 128, p_b0[:])
+        scatter(2, 0, 128, p_head[2][:])
+        c0_bank = bank(0)
+        second_product(c0_bank[:, 0:256], 0, 256, 256)
+        p_c0 = sb.tile([P, 256], F32)
+        leave(p_c0[:], c0_bank[:, 0:256], 0)
+        rest = {}
+        for n in (1, 2):
+            rest_bank = bank(n)
+            second_product(rest_bank[:, 0:128], n, 128, 128)
+            second_product(rest_bank[:, 128:384], n, 256, 256)
+            rest[n] = sb.tile([P, 384], F32, name="p_rest%d" % n)
+            leave(rest[n][:], rest_bank[:, 0:384], n)
+        last_bank = bank(3)
+        second_product(last_bank[:], 3, 0, 512)
+        p_last = sb.tile([P, I], F32)
+        leave(p_last[:], last_bank[:], 3)
+
+        def turn(dst, src, start, stop):
+            nc.tensor.matmul(dst, src, ident[:], start=start, stop=stop, is_transpose=True)
+
+        sum_banks = {0: (6, 7), 1: (1, 2), 2: (3, 0)}
+        back_banks = {0: (4, 5), 1: (6, 7), 2: (4, 5)}
+        opened = {}
+
+        def open_sum(n):
+            opened[n] = [bank(b) for b in sum_banks[n]]
+            for h in range(2):
+                for b in range(4):
+                    cols = slice(BANK * h + P * b, BANK * h + P * (b + 1))
+                    turn(opened[n][h][:, P * b : P * (b + 1)], old_sb[n // 2][:, n % 2, cols], b == 0, False)
+
+        def close_sum(n):
+            for h in range(2):
+                for b in range(4):
+                    cols = slice(BANK * h + P * b, BANK * h + P * (b + 1))
+                    turn(opened[n][h][:, P * b : P * (b + 1)], places[n][:, cols], False, b == 3)
+            turned = []
+            for h in range(2):
+                turned.append(sb.tile([P, BANK], F32, name="turned", tag="turned", bufs=4))
+                nc.scalar.copy(turned[h][:], opened[n][h][:])
+            for h in range(2):
+                back = bank(back_banks[n][h])
+                for b in range(4):
+                    turn(back[:, P * b : P * (b + 1)], turned[h][:, P * b : P * (b + 1)], True, True)
+                result = sb.tile([P, BANK], F32, name="result", tag="result", bufs=4)
+                nc.scalar.activation(result[:], back[:], ACT.Copy, scale=OLD_WEIGHT)
+                nc.sync.dma_start(out[P * n : P * (n + 1), BANK * h : BANK * (h + 1)], result[:])
+
+        open_sum(0)
+        scatter(0, 256, 256, p_c0[:])
+        open_sum(1)
+        close_sum(0)
+        scatter(1, 128, 384, rest[1][:])
+        open_sum(2)
+        close_sum(1)
+        scatter(2, 128, 384, rest[2][:])
+        close_sum(2)
+        scatter(3, 0, 512, p_last[:])
+        for h in range(2):
+            cols = slice(BANK * h, BANK * (h + 1))
+            result = sb.tile([P, BANK], F32, name="result", tag="result", bufs=4)
+            nc.vector.scalar_tensor_tensor(
+                result[:], old_sb[1][:, 1, cols], OLD_WEIGHT, places[3][:, cols], ALU.mult, ALU.add
+            )
+            nc.sync.dma_start(out[3 * P : 4 * P, cols], result[:])

@@ -38,7 +38,7 @@ def tile_moe_expert_relay_scattered_kernel(
         def entries(tile, first, count):
             return tile[:, first // 16 : (first + count) // 16]
 
-        wa_planes_raw = sb.tile([P, 2 * R], U8, align_bytes=64)
+        wa_planes_raw = sb.tile([P, 2 * R], U8, tag="wb_planes", align_bytes=64)
         nc.vector.memset(wa_planes_raw[:].bitcast(I32), 0)
         x_rows = sb.tile([P, T], U8, align_bytes=64)
         nc.vector.memset(x_rows[0:96, :].bitcast(I32), 0)
@@ -65,14 +65,12 @@ def tile_moe_expert_relay_scattered_kernel(
 
         xg_plane = [sb.tile([P, J], U8, name="xg_plane%d" % z, align_bytes=64) for z in range(2)]
         for z in range(2):
-            nc.gpsimd.memset(xg_plane[z][:].bitcast(I32), 0)
+            nc.vector.memset(xg_plane[z][:].bitcast(I32), 0)
         places = [sb.tile([P, S], F32, name="places%d" % n) for n in range(2)]
         for n in range(2):
-            nc.gpsimd.memset(places[n][:], 0.0)
+            nc.vector.memset(places[n][:], 0.0)
         ident = sb.tile([P, P], F32)
         make_identity(nc, ident[:])
-        wb_planes = sb.tile([P, N], U8, align_bytes=64)
-        nc.gpsimd.memset(wb_planes[:].bitcast(I32), 0)
 
         xg_rows = sb.tile([P, J], U8, align_bytes=64)
         nc.vector.tensor_copy(xg_rows[:], x_rows[:].indirect(idx[:]))
@@ -82,11 +80,6 @@ def tile_moe_expert_relay_scattered_kernel(
                 nc.scalar.dma_start(
                     xg_plane[z][32 * q : 32 * q + 4, :].bitcast(I32), xg_rows[first : first + 4, :].bitcast(I32)
                 )
-
-        for q in range(4):
-            nc.sync.dma_start(
-                wb_planes[32 * q : 32 * q + 4, :].bitcast(I32), wb_scales[0, 4 * q : 4 * q + 4, :].bitcast(I32)
-            )
 
         wa_codes = sb.tile([P, 2, 2 * R], U8, align_bytes=64)
         nc.vector.tensor_copy(
@@ -101,6 +94,13 @@ def tile_moe_expert_relay_scattered_kernel(
 
         wb_codes = sb.tile([P, N], I32, tag="wb", align_bytes=64)
         nc.sync.dma_start(wb_codes[:], wb_words[0].rearrange("p c r -> p (c r)").bitcast(I32))
+
+        wb_planes = sb.tile([P, N], U8, tag="wb_planes", align_bytes=64)
+        nc.vector.memset(wb_planes[:].bitcast(I32), 0)
+        for q in range(4):
+            nc.sync.dma_start(
+                wb_planes[32 * q : 32 * q + 4, :].bitcast(I32), wb_scales[0, 4 * q : 4 * q + 4, :].bitcast(I32)
+            )
 
         xg = [[sb.tile([P, BANK], U32, name="xg%d%d" % (z, h), tag="old_b" if z + h == 0 else "xg%d%d" % (z, h), align_bytes=64) for h in range(2)] for z in range(2)]
         acc = {}
@@ -155,10 +155,8 @@ def tile_moe_expert_relay_scattered_kernel(
 
         def interleave(first, count):
             nc.scalar.copy(
-                grouped[:, 4 * first : 4 * (first + count)].rearrange("p (c i t) -> p c t i", i=4, t=4),
-                picked[:].rearrange("p (t c) -> p t c", t=4)[:, :, first : first + count].rearrange(
-                    "p t (c i) -> p c t i", i=4
-                ),
+                grouped[:, 4 * first : 4 * (first + count)].rearrange("p (c t) -> p c t", t=4),
+                picked[:].rearrange("p (t c) -> p c t", t=4)[:, first : first + count, :],
             )
 
         def quantise(first, count):

@@ -189,35 +189,35 @@ def tile_moe_expert_relay_scattered_kernel(
         quantise(0, 128)
         interleave(128, 128)
         head_bank = bank(4)
-        p_head = [sb.tile([P, P], F32, name="p_head%d" % n) for n in range(3)]
+        p_head01 = sb.tile([P, 2 * P], F32)
+        p_head2 = sb.tile([P, P], F32)
         for n in range(3):
             second_product(head_bank[:, P * n : P * (n + 1)], n, 0, 128)
-        for n in range(2):
-            leave(p_head[n][:], head_bank[:, P * n : P * (n + 1)], n)
         quantise(128, 128)
+        nc.vector.tensor_scalar_mul(p_head01[:], head_bank[:, 0 : 2 * P], 1.0 / OLD_WEIGHT)
         interleave(256, 256)
-        leave(p_head[2][:], head_bank[:, 2 * P : 3 * P], 2)
+        leave(p_head2[:], head_bank[:, 2 * P : 3 * P], 2)
         b0_bank = bank(5)
         second_product(b0_bank[:, 0:128], 0, 128, 128)
         p_b0 = sb.tile([P, 128], F32)
         leave(p_b0[:], b0_bank[:, 0:128], 0)
-        scatter(0, 0, 128, p_head[0][:])
-        scatter(1, 0, 128, p_head[1][:])
+        scatter(0, 0, 128, p_head01[:, 0:P])
+        scatter(1, 0, 128, p_head01[:, P : 2 * P])
         quantise(256, 256)
         scatter(0, 128, 128, p_b0[:])
-        scatter(2, 0, 128, p_head[2][:])
-        c0_bank = bank(0)
+        scatter(2, 0, 128, p_head2[:])
+        c0_bank = bank(6)
         second_product(c0_bank[:, 0:256], 0, 256, 256)
         p_c0 = sb.tile([P, 256], F32)
         leave(p_c0[:], c0_bank[:, 0:256], 0)
         rest = {}
         for n in (1, 2):
-            rest_bank = bank(n)
+            rest_bank = bank(7 if n == 1 else 4)
             second_product(rest_bank[:, 0:128], n, 128, 128)
             second_product(rest_bank[:, 128:384], n, 256, 256)
             rest[n] = sb.tile([P, 384], F32, name="p_rest%d" % n)
             leave(rest[n][:], rest_bank[:, 0:384], n)
-        last_bank = bank(3)
+        last_bank = bank(5)
         second_product(last_bank[:], 3, 0, 512)
         p_last = sb.tile([P, I], F32)
         leave(p_last[:], last_bank[:], 3)
@@ -225,8 +225,8 @@ def tile_moe_expert_relay_scattered_kernel(
         def turn(dst, src, start, stop):
             nc.tensor.matmul(dst, src, ident[:], start=start, stop=stop, is_transpose=True)
 
-        sum_banks = {0: (6, 7), 1: (1, 2), 2: (3, 0)}
-        back_banks = {0: (4, 5), 1: (6, 7), 2: (4, 5)}
+        sum_banks = {0: (2, 3), 1: (0, 1), 2: (6, 7)}
+        back_banks = {0: (4, 5), 1: (2, 3), 2: (0, 1)}
         opened = {}
 
         def open_sum(n):
@@ -243,29 +243,29 @@ def tile_moe_expert_relay_scattered_kernel(
                     turn(opened[n][h][:, P * b : P * (b + 1)], places[n][:, cols], False, b == 3)
             turned = []
             for h in range(2):
-                turned.append(sb.tile([P, BANK], F32, name="turned", tag="turned", bufs=4))
+                turned.append(sb.tile([P, BANK], F32, name="turned", tag="turned%d" % n, bufs=2))
                 nc.scalar.copy(turned[h][:], opened[n][h][:])
             for h in range(2):
                 back = bank(back_banks[n][h])
                 for b in range(4):
                     turn(back[:, P * b : P * (b + 1)], turned[h][:, P * b : P * (b + 1)], True, True)
-                result = sb.tile([P, BANK], F32, name="result", tag="result", bufs=4)
+                result = sb.tile([P, BANK], F32, name="result", tag="result", bufs=6)
                 nc.scalar.activation(result[:], back[:], ACT.Copy, scale=OLD_WEIGHT)
                 nc.sync.dma_start(out[P * n : P * (n + 1), BANK * h : BANK * (h + 1)], result[:])
 
-        open_sum(0)
-        scatter(0, 256, 256, p_c0[:])
         open_sum(1)
+        open_sum(0)
+        open_sum(2)
+        scatter(0, 256, 256, p_c0[:])
         close_sum(0)
         scatter(1, 128, 384, rest[1][:])
-        open_sum(2)
         close_sum(1)
         scatter(2, 128, 384, rest[2][:])
         close_sum(2)
         scatter(3, 0, 512, p_last[:])
         for h in range(2):
             cols = slice(BANK * h, BANK * (h + 1))
-            result = sb.tile([P, BANK], F32, name="result", tag="result", bufs=4)
+            result = sb.tile([P, BANK], F32, name="last_result", tag="turned2", bufs=2)
             nc.vector.scalar_tensor_tensor(
                 result[:], old_sb[1][:, 1, cols], OLD_WEIGHT, places[3][:, cols], ALU.mult, ALU.add
             )

@@ -20,6 +20,8 @@ ALU = mybir.AluOpType
 P = 128
 BANK = 512
 OLD_WEIGHT = 0.3
+CHUNK_A, CHUNK_B, CHUNK_C = (0, 128), (128, 128), (256, 256)
+TAIL = ((2, 512, 512), (3, 0, 512), (3, 512, 256), (3, 768, 256))
 
 
 def tile_moe_expert_relay_scattered_kernel(
@@ -29,29 +31,29 @@ def tile_moe_expert_relay_scattered_kernel(
     with ExitStack() as ctx:
         lists = ctx.enter_context(tc.tile_pool(name="lists", bufs=1))
         sb = ctx.enter_context(tc.tile_pool(name="sb", bufs=1))
-        late = ctx.enter_context(tc.tile_pool(name="late", bufs=1))
+        shared = ctx.enter_context(tc.tile_pool(name="shared", bufs=1))
         psum = ctx.enter_context(tc.psum_pool(name="psum", bufs=1))
 
         def bank(b):
             return psum.tile([P, BANK], F32, name="bank%d" % b, tag="bank%d" % b)
 
-        def entries(tile, first, count):
-            return tile[:, first // 16 : (first + count) // 16]
+        def entries(list_tile, first, count):
+            return list_tile[:, first // 16 : (first + count) // 16]
 
-        wa_planes_raw = sb.tile([P, 2 * R], U8, tag="wb_planes", align_bytes=64)
+        wa_planes_raw = sb.tile([P, 2 * R], U8, tag="wb_plane", align_bytes=64)
         nc.vector.memset(wa_planes_raw[:].bitcast(I32), 0)
         x_rows = sb.tile([P, T], U8, align_bytes=64)
         nc.vector.memset(x_rows[0:96, :].bitcast(I32), 0)
         nc.sync.dma_start(x_rows[96:128, :].bitcast(I32), xt_scales.rearrange("z q c -> (z q) c").bitcast(I32))
         idx = lists.tile([P, J // 16], U16)
         nc.sync.dma_start(idx[:], offs)
-        wa_raw = sb.tile([P, 2, 2 * R], U8, tag="wb", align_bytes=64)
+        wa_raw = sb.tile([P, 2, 2 * R], U8, tag="wb_codes", align_bytes=64)
         nc.sync.dma_start(wa_raw[:].bitcast(I32), wa_words.rearrange("z p c -> p z c").bitcast(I32))
-        x_win = [
-            sb.tile([P, T], I32, name="x_win0", tag="old_a", align_bytes=64),
-            late.tile([P, T], I32, name="x_win1", offset=0),
+        x_words = [
+            sb.tile([P, T], I32, name="x_words0", tag="old0", align_bytes=64),
+            shared.tile([P, T], I32, name="x_words1", offset=0),
         ]
-        nc.sync.dma_start(x_win[0][:], xt_words[0].rearrange("p c r -> p (c r)").bitcast(I32))
+        nc.sync.dma_start(x_words[0][:], xt_words[0].rearrange("p c r -> p (c r)").bitcast(I32))
         idx2 = lists.tile([P, I // 16], U16)
         nc.sync.dma_start(idx2[:], offs2)
         idx3 = lists.tile([P, I // 16], U16)
@@ -61,7 +63,7 @@ def tile_moe_expert_relay_scattered_kernel(
                 wa_planes_raw[32 * q : 32 * q + 4, :].bitcast(I32).rearrange("p (z c) -> p z c", z=2),
                 wa_scales[:, 4 * q : 4 * q + 4, :].rearrange("z q c -> q z c").bitcast(I32),
             )
-        nc.sync.dma_start(x_win[1][:], xt_words[1].rearrange("p c r -> p (c r)").bitcast(I32))
+        nc.sync.dma_start(x_words[1][:], xt_words[1].rearrange("p c r -> p (c r)").bitcast(I32))
 
         xg_plane = [sb.tile([P, J], U8, name="xg_plane%d" % z, align_bytes=64) for z in range(2)]
         for z in range(2):
@@ -76,9 +78,9 @@ def tile_moe_expert_relay_scattered_kernel(
         nc.vector.tensor_copy(xg_rows[:], x_rows[:].indirect(idx[:]))
         for z in range(2):
             for q in range(4):
-                first = 96 + 16 * z + 4 * q
+                row = 96 + 16 * z + 4 * q
                 nc.scalar.dma_start(
-                    xg_plane[z][32 * q : 32 * q + 4, :].bitcast(I32), xg_rows[first : first + 4, :].bitcast(I32)
+                    xg_plane[z][32 * q : 32 * q + 4, :].bitcast(I32), xg_rows[row : row + 4, :].bitcast(I32)
                 )
 
         wa_codes = sb.tile([P, 2, 2 * R], U8, align_bytes=64)
@@ -92,23 +94,23 @@ def tile_moe_expert_relay_scattered_kernel(
             wa_planes_raw[:].rearrange("p (z b i t) -> p z b t i", z=2, t=4, i=16),
         )
 
-        wb_codes = sb.tile([P, N], I32, tag="wb", align_bytes=64)
+        wb_codes = sb.tile([P, N], I32, tag="wb_codes", align_bytes=64)
         nc.sync.dma_start(wb_codes[:], wb_words[0].rearrange("p c r -> p (c r)").bitcast(I32))
-
-        wb_planes = sb.tile([P, N], U8, tag="wb_planes", align_bytes=64)
-        nc.vector.memset(wb_planes[:].bitcast(I32), 0)
+        wb_plane = sb.tile([P, N], U8, tag="wb_plane", align_bytes=64)
+        nc.vector.memset(wb_plane[:].bitcast(I32), 0)
         for q in range(4):
             nc.sync.dma_start(
-                wb_planes[32 * q : 32 * q + 4, :].bitcast(I32), wb_scales[0, 4 * q : 4 * q + 4, :].bitcast(I32)
+                wb_plane[32 * q : 32 * q + 4, :].bitcast(I32), wb_scales[0, 4 * q : 4 * q + 4, :].bitcast(I32)
             )
 
-        xg = [[sb.tile([P, BANK], U32, name="xg%d%d" % (z, h), tag="old_b" if z + h == 0 else "xg%d%d" % (z, h), align_bytes=64) for h in range(2)] for z in range(2)]
+        xg_tags = (("old1", "xg01"), ("xg10", "xg11"))
+        xg = [[sb.tile([P, BANK], U32, name="xg", tag=tag, align_bytes=64) for tag in tags] for tags in xg_tags]
         acc = {}
 
         def first_product(t, z, h):
             nc.tensor.matmul_mx(
                 out=acc[t, h][:],
-                lhsT=wa_codes[:, z, 256 * t : 256 * (t + 1)].bitcast(FP4X4),
+                lhsT=wa_codes[:, z, 2 * P * t : 2 * P * (t + 1)].bitcast(FP4X4),
                 lhsT_scale=wa_planes[:, R * z + P * t : R * z + P * (t + 1)],
                 rhs=xg[z][h][:].bitcast(FP8X4),
                 rhs_scale=xg_plane[z][:, BANK * h : BANK * (h + 1)],
@@ -118,18 +120,18 @@ def tile_moe_expert_relay_scattered_kernel(
 
         for z in range(2):
             for h in range(2):
-                nc.vector.tensor_copy(xg[z][h][:], x_win[z][:].bitcast(U32).indirect(entries(idx, BANK * h, BANK)))
+                nc.vector.tensor_copy(xg[z][h][:], x_words[z][:].bitcast(U32).indirect(entries(idx, BANK * h, BANK)))
         for h in range(2):
             for t in range(2):
                 acc[t, h] = bank(2 * t + h)
                 first_product(t, 0, h)
 
-        old_sb = [sb.tile([P, 2, S], F32, name="old_" + c, tag="old_" + c, align_bytes=64) for c in "ab"]
+        old_pair = [sb.tile([P, 2, S], F32, name="old%d" % c, tag="old%d" % c, align_bytes=64) for c in range(2)]
         for c in range(2):
-            nc.sync.dma_start(old_sb[c][:], old[256 * c : 256 * (c + 1), :].rearrange("(n p) s -> p n s", n=2))
+            nc.sync.dma_start(old_pair[c][:], old[2 * P * c : 2 * P * (c + 1), :].rearrange("(b p) s -> p b s", b=2))
 
         for n in (2, 3):
-            places.append(late.tile([P, S], F32, name="places%d" % n, offset=4 * S * (n - 2)))
+            places.append(shared.tile([P, S], F32, name="places%d" % n, offset=4 * S * (n - 2)))
             nc.vector.memset(places[n][:], 0.0)
 
         hid = [sb.tile([P, J], F32, name="hid%d" % t) for t in range(4)]
@@ -142,21 +144,19 @@ def tile_moe_expert_relay_scattered_kernel(
                 nc.scalar.activation(hid[t][:, BANK * h : BANK * (h + 1)], acc[t, h][:], ACT.Relu)
 
         picked = sb.tile([P, 4 * I], F32)
-        for t in range(3):
-            nc.vector.tensor_copy(picked[:, I * t : I * (t + 1)], hid[t][:].indirect(idx2[:]))
         grouped = sb.tile([P, 4 * I], BF16, align_bytes=64)
         h_codes = sb.tile([P, I], U32, align_bytes=64)
         h_plane = sb.tile([P, I], U8, align_bytes=64)
 
-        def gather_last(first, count):
+        def gather_hid(t, first, count):
             nc.vector.tensor_copy(
-                picked[:, 3 * I + first : 3 * I + first + count], hid[3][:].indirect(entries(idx2, first, count))
+                picked[:, I * t + first : I * t + first + count], hid[t][:].indirect(entries(idx2, first, count))
             )
 
         def interleave(first, count):
             nc.scalar.copy(
-                grouped[:, 4 * first : 4 * (first + count)].rearrange("p (c t) -> p c t", t=4),
-                picked[:].rearrange("p (t c) -> p c t", t=4)[:, first : first + count, :],
+                grouped[:, 4 * first : 4 * (first + count)].rearrange("p (i t) -> p i t", t=4),
+                picked[:].rearrange("p (t i) -> p i t", t=4)[:, first : first + count, :],
             )
 
         def quantise(first, count):
@@ -170,103 +170,106 @@ def tile_moe_expert_relay_scattered_kernel(
             nc.tensor.matmul_mx(
                 out=dst,
                 lhsT=wb_codes[:, P * n : P * (n + 1)].bitcast(FP8X4),
-                lhsT_scale=wb_planes[:, P * n : P * (n + 1)],
+                lhsT_scale=wb_plane[:, P * n : P * (n + 1)],
                 rhs=h_codes[:, first : first + count].bitcast(FP8X4),
                 rhs_scale=h_plane[:, first : first + count],
                 start=True,
                 stop=True,
             )
 
-        def leave(dst, src, n):
-            nc.scalar.activation(dst, src, ACT.Copy, scale=1.0 / OLD_WEIGHT if n < 3 else 1.0)
-
         def scatter(n, first, count, src):
             nc.vector.tensor_copy(places[n][:].indirect(entries(idx3, first, count)), src)
 
-        gather_last(0, 128)
-        interleave(0, 128)
-        gather_last(128, 384)
-        quantise(0, 128)
-        interleave(128, 128)
-        head_bank = bank(4)
-        p_head01 = sb.tile([P, 2 * P], F32)
-        p_head2 = sb.tile([P, P], F32)
-        for n in range(3):
-            second_product(head_bank[:, P * n : P * (n + 1)], n, 0, 128)
-        quantise(128, 128)
-        nc.vector.tensor_scalar_mul(p_head01[:], head_bank[:, 0 : 2 * P], 1.0 / OLD_WEIGHT)
-        interleave(256, 256)
-        leave(p_head2[:], head_bank[:, 2 * P : 3 * P], 2)
-        b0_bank = bank(5)
-        second_product(b0_bank[:, 0:128], 0, 128, 128)
-        p_b0 = sb.tile([P, 128], F32)
-        leave(p_b0[:], b0_bank[:, 0:128], 0)
-        scatter(0, 0, 128, p_head01[:, 0:P])
-        scatter(1, 0, 128, p_head01[:, P : 2 * P])
-        quantise(256, 256)
-        scatter(0, 128, 128, p_b0[:])
-        scatter(2, 0, 128, p_head2[:])
-        c0_bank = bank(6)
-        second_product(c0_bank[:, 0:256], 0, 256, 256)
-        p_c0 = sb.tile([P, 256], F32)
-        leave(p_c0[:], c0_bank[:, 0:256], 0)
-        rest = {}
-        for n in (1, 2):
-            rest_bank = bank(7 if n == 1 else 4)
-            second_product(rest_bank[:, 0:128], n, 128, 128)
-            second_product(rest_bank[:, 128:384], n, 256, 256)
-            rest[n] = sb.tile([P, 384], F32, name="p_rest%d" % n)
-            leave(rest[n][:], rest_bank[:, 0:384], n)
-        last_bank = bank(5)
-        second_product(last_bank[:], 3, 0, 512)
-        p_last = sb.tile([P, I], F32)
-        leave(p_last[:], last_bank[:], 3)
+        for t in range(3):
+            gather_hid(t, 0, I)
+        gather_hid(3, *CHUNK_A)
+        interleave(*CHUNK_A)
+        gather_hid(3, CHUNK_B[0], I - CHUNK_B[0])
+        quantise(*CHUNK_A)
+        interleave(*CHUNK_B)
+        bank_a = bank(4)
+        for n in range(2):
+            second_product(bank_a[:, P * n : P * (n + 1)], n, *CHUNK_A)
+        quantise(*CHUNK_B)
+        p_a = sb.tile([P, 2 * P], F32)
+        nc.vector.tensor_scalar_mul(p_a[:], bank_a[:, 0 : 2 * P], 1.0 / OLD_WEIGHT)
+        interleave(*CHUNK_C)
+        bank_b = bank(5)
+        for n in range(2):
+            second_product(bank_b[:, P * n : P * (n + 1)], n, *CHUNK_B)
+        p_b = sb.tile([P, 2 * P], F32)
+        nc.scalar.activation(p_b[:], bank_b[:, 0 : 2 * P], ACT.Copy, scale=1.0 / OLD_WEIGHT)
+        for n in range(2):
+            scatter(n, *CHUNK_A, p_a[:, P * n : P * (n + 1)])
+        quantise(*CHUNK_C)
+        for n in range(2):
+            scatter(n, *CHUNK_B, p_b[:, P * n : P * (n + 1)])
+        p_c = []
+        for n in range(2):
+            bank_c = bank(6 + n)
+            second_product(bank_c[:, 0 : 2 * P], n, *CHUNK_C)
+            p_c.append(sb.tile([P, 2 * P], F32, name="p_c%d" % n, tag="p_c%d" % n))
+            nc.scalar.activation(p_c[n][:], bank_c[:, 0 : 2 * P], ACT.Copy, scale=1.0 / OLD_WEIGHT)
+        p_whole = {}
+        for n in (2, 3):
+            bank_whole = bank(2 + n)
+            second_product(bank_whole[:], n, 0, I)
+            p_whole[n] = sb.tile([P, I], F32, name="p_whole%d" % n)
+            nc.scalar.activation(p_whole[n][:], bank_whole[:], ACT.Copy, scale=1.0)
+
+        sum_banks = {0: (2, 3), 1: (0, 1), 2: (1,)}
+        back_banks = {0: (6, 7), 1: (2, 3), 2: (4,)}
+        sums = {}
 
         def turn(dst, src, start, stop):
             nc.tensor.matmul(dst, src, ident[:], start=start, stop=stop, is_transpose=True)
 
-        sum_banks = {0: (2, 3), 1: (0, 1), 2: (6, 7)}
-        back_banks = {0: (4, 5), 1: (2, 3), 2: (0, 1)}
-        opened = {}
-
-        def open_sum(n):
-            opened[n] = [bank(b) for b in sum_banks[n]]
-            for h in range(2):
+        def open_sum(n, addend):
+            sums[n] = [bank(b) for b in sum_banks[n]]
+            for h in range(len(sums[n])):
                 for b in range(4):
                     cols = slice(BANK * h + P * b, BANK * h + P * (b + 1))
-                    turn(opened[n][h][:, P * b : P * (b + 1)], old_sb[n // 2][:, n % 2, cols], b == 0, False)
+                    turn(sums[n][h][:, P * b : P * (b + 1)], addend[:, cols], b == 0, False)
 
-        def close_sum(n):
-            for h in range(2):
+        def close_sum(n, factor):
+            halves = range(len(sums[n]))
+            for h in halves:
                 for b in range(4):
                     cols = slice(BANK * h + P * b, BANK * h + P * (b + 1))
-                    turn(opened[n][h][:, P * b : P * (b + 1)], places[n][:, cols], False, b == 3)
+                    turn(sums[n][h][:, P * b : P * (b + 1)], places[n][:, cols], False, b == 3)
             turned = []
-            for h in range(2):
-                turned.append(sb.tile([P, BANK], F32, name="turned", tag="turned%d" % n, bufs=2))
-                nc.scalar.copy(turned[h][:], opened[n][h][:])
-            for h in range(2):
+            for h in halves:
+                turned.append(sb.tile([P, BANK], F32, name="turned%d%d" % (n, h), tag="turned%d%d" % (n, h)))
+                nc.scalar.copy(turned[h][:], sums[n][h][:])
+            for h in halves:
                 back = bank(back_banks[n][h])
                 for b in range(4):
                     turn(back[:, P * b : P * (b + 1)], turned[h][:, P * b : P * (b + 1)], True, True)
-                result = sb.tile([P, BANK], F32, name="result", tag="result", bufs=6)
-                nc.scalar.activation(result[:], back[:], ACT.Copy, scale=OLD_WEIGHT)
-                nc.sync.dma_start(out[P * n : P * (n + 1), BANK * h : BANK * (h + 1)], result[:])
+                result = sb.tile([P, BANK], F32, name="result%d%d" % (n, h))
+                nc.scalar.activation(result[:], back[:], ACT.Copy, scale=factor)
+                queue = nc.sync if 2 * n + h < 3 else nc.scalar
+                queue.dma_start(out[P * n : P * (n + 1), BANK * h : BANK * (h + 1)], result[:])
 
-        open_sum(1)
-        open_sum(0)
-        open_sum(2)
-        scatter(0, 256, 256, p_c0[:])
-        close_sum(0)
-        scatter(1, 128, 384, rest[1][:])
-        close_sum(1)
-        scatter(2, 128, 384, rest[2][:])
-        close_sum(2)
-        scatter(3, 0, 512, p_last[:])
-        for h in range(2):
-            cols = slice(BANK * h, BANK * (h + 1))
-            result = sb.tile([P, BANK], F32, name="last_result", tag="turned2", bufs=2)
+        open_sum(1, old_pair[0][:, 1, :])
+        open_sum(0, old_pair[0][:, 0, :])
+        scatter(0, *CHUNK_C, p_c[0][:])
+        old_scaled = sb.tile([P, BANK], F32, tag="p_c0")
+        nc.scalar.activation(old_scaled[:], old_pair[1][:, 0, 0:BANK], ACT.Copy, scale=OLD_WEIGHT)
+        close_sum(0, OLD_WEIGHT)
+        scatter(1, *CHUNK_C, p_c[1][:])
+        close_sum(1, OLD_WEIGHT)
+        open_sum(2, old_scaled[:])
+        scatter(2, 0, I, p_whole[2][:])
+        close_sum(2, 1.0)
+        scatter(3, 0, I, p_whole[3][:])
+
+        tail = sb.tile([P, 3 * BANK], F32, tag="turned11")
+        done = 0
+        for n, first, count in TAIL:
+            cols = slice(first, first + count)
+            result = tail[:, done : done + count]
             nc.vector.scalar_tensor_tensor(
-                result[:], old_sb[1][:, 1, cols], OLD_WEIGHT, places[3][:, cols], ALU.mult, ALU.add
+                result, old_pair[1][:, n - 2, cols], OLD_WEIGHT, places[n][:, cols], ALU.mult, ALU.add
             )
-            nc.sync.dma_start(out[3 * P : 4 * P, cols], result[:])
+            nc.sync.dma_start(out[P * n : P * (n + 1), cols], result)
+            done = done + count

from contextlib import ExitStack

import concourse.mybir as mybir
from concourse.masks import make_identity

K, T, J, I, S, R, N = 1024, 2048, 1024, 512, 1024, 512, 512
FLOPS = 2 * K * R * J + 2 * R * N * I

F32 = mybir.dt.float32
BF16 = mybir.dt.bfloat16
I32 = mybir.dt.int32
U32 = mybir.dt.uint32
U16 = mybir.dt.uint16
U8 = mybir.dt.uint8
FP8X4 = mybir.dt.float8_e4m3fn_x4
FP4X4 = mybir.dt.float4_e2m1fn_x4
ACT = mybir.ActivationFunctionType
ALU = mybir.AluOpType

P = 128
BANK = 512
OLD_WEIGHT = 0.3
CHUNK_A, CHUNK_B, CHUNK_C = (0, 128), (128, 128), (256, 256)
TAIL = ((2, 512, 512), (3, 0, 512), (3, 512, 256), (3, 768, 256))


def tile_moe_expert_relay_scattered_kernel(
    tc, xt_words, xt_scales, wa_words, wa_scales, wb_words, wb_scales, old, offs, offs2, offs3, out
):
    nc = tc.nc
    with ExitStack() as ctx:
        lists = ctx.enter_context(tc.tile_pool(name="lists", bufs=1))
        sb = ctx.enter_context(tc.tile_pool(name="sb", bufs=1))
        shared = ctx.enter_context(tc.tile_pool(name="shared", bufs=1))
        psum = ctx.enter_context(tc.psum_pool(name="psum", bufs=1))

        def bank(b):
            return psum.tile([P, BANK], F32, name="bank%d" % b, tag="bank%d" % b)

        def entries(list_tile, first, count):
            return list_tile[:, first // 16 : (first + count) // 16]

        wa_planes_raw = sb.tile([P, 2 * R], U8, tag="wb_plane", align_bytes=64)
        nc.vector.memset(wa_planes_raw[:].bitcast(I32), 0)
        x_rows = sb.tile([P, T], U8, align_bytes=64)
        nc.vector.memset(x_rows[0:96, :].bitcast(I32), 0)
        nc.sync.dma_start(x_rows[96:128, :].bitcast(I32), xt_scales.rearrange("z q c -> (z q) c").bitcast(I32))
        idx = lists.tile([P, J // 16], U16)
        nc.sync.dma_start(idx[:], offs)
        wa_raw = sb.tile([P, 2, 2 * R], U8, tag="wb_codes", align_bytes=64)
        nc.sync.dma_start(wa_raw[:].bitcast(I32), wa_words.rearrange("z p c -> p z c").bitcast(I32))
        x_words = [
            sb.tile([P, T], I32, name="x_words0", tag="old0", align_bytes=64),
            shared.tile([P, T], I32, name="x_words1", offset=0),
        ]
        nc.sync.dma_start(x_words[0][:], xt_words[0].rearrange("p c r -> p (c r)").bitcast(I32))
        idx2 = lists.tile([P, I // 16], U16)
        nc.sync.dma_start(idx2[:], offs2)
        idx3 = lists.tile([P, I // 16], U16)
        nc.sync.dma_start(idx3[:], offs3)
        for q in range(4):
            nc.sync.dma_start(
                wa_planes_raw[32 * q : 32 * q + 4, :].bitcast(I32).rearrange("p (z c) -> p z c", z=2),
                wa_scales[:, 4 * q : 4 * q + 4, :].rearrange("z q c -> q z c").bitcast(I32),
            )
        nc.sync.dma_start(x_words[1][:], xt_words[1].rearrange("p c r -> p (c r)").bitcast(I32))

        xg_plane = [sb.tile([P, J], U8, name="xg_plane%d" % z, align_bytes=64) for z in range(2)]
        for z in range(2):
            nc.vector.memset(xg_plane[z][:].bitcast(I32), 0)
        places = [sb.tile([P, S], F32, name="places%d" % n) for n in range(2)]
        for n in range(2):
            nc.vector.memset(places[n][:], 0.0)
        ident = sb.tile([P, P], F32)
        make_identity(nc, ident[:])

        xg_rows = sb.tile([P, J], U8, align_bytes=64)
        nc.vector.tensor_copy(xg_rows[:], x_rows[:].indirect(idx[:]))
        for z in range(2):
            for q in range(4):
                row = 96 + 16 * z + 4 * q
                nc.scalar.dma_start(
                    xg_plane[z][32 * q : 32 * q + 4, :].bitcast(I32), xg_rows[row : row + 4, :].bitcast(I32)
                )

        wa_codes = sb.tile([P, 2, 2 * R], U8, align_bytes=64)
        nc.vector.tensor_copy(
            wa_codes[:].bitcast(U16).rearrange("p z (t b i) -> p z b t i", t=4, i=8),
            wa_raw[:].bitcast(U16).rearrange("p z (b i t) -> p z b t i", t=4, i=8),
        )
        wa_planes = sb.tile([P, 2 * R], U8, align_bytes=64)
        nc.vector.tensor_copy(
            wa_planes[:].rearrange("p (z t b i) -> p z b t i", z=2, t=4, i=16),
            wa_planes_raw[:].rearrange("p (z b i t) -> p z b t i", z=2, t=4, i=16),
        )

        wb_codes = sb.tile([P, N], I32, tag="wb_codes", align_bytes=64)
        nc.sync.dma_start(wb_codes[:], wb_words[0].rearrange("p c r -> p (c r)").bitcast(I32))
        wb_plane = sb.tile([P, N], U8, tag="wb_plane", align_bytes=64)
        nc.vector.memset(wb_plane[:].bitcast(I32), 0)
        for q in range(4):
            nc.sync.dma_start(
                wb_plane[32 * q : 32 * q + 4, :].bitcast(I32), wb_scales[0, 4 * q : 4 * q + 4, :].bitcast(I32)
            )

        xg_tags = (("old1", "xg01"), ("xg10", "xg11"))
        xg = [[sb.tile([P, BANK], U32, name="xg", tag=tag, align_bytes=64) for tag in tags] for tags in xg_tags]
        acc = {}

        def first_product(t, z, h):
            nc.tensor.matmul_mx(
                out=acc[t, h][:],
                lhsT=wa_codes[:, z, 2 * P * t : 2 * P * (t + 1)].bitcast(FP4X4),
                lhsT_scale=wa_planes[:, R * z + P * t : R * z + P * (t + 1)],
                rhs=xg[z][h][:].bitcast(FP8X4),
                rhs_scale=xg_plane[z][:, BANK * h : BANK * (h + 1)],
                start=(z == 0),
                stop=(z == 1),
            )

        for z in range(2):
            for h in range(2):
                nc.vector.tensor_copy(xg[z][h][:], x_words[z][:].bitcast(U32).indirect(entries(idx, BANK * h, BANK)))
        for h in range(2):
            for t in range(2):
                acc[t, h] = bank(2 * t + h)
                first_product(t, 0, h)

        old_pair = [sb.tile([P, 2, S], F32, name="old%d" % c, tag="old%d" % c, align_bytes=64) for c in range(2)]
        for c in range(2):
            nc.sync.dma_start(old_pair[c][:], old[2 * P * c : 2 * P * (c + 1), :].rearrange("(b p) s -> p b s", b=2))

        for n in (2, 3):
            places.append(shared.tile([P, S], F32, name="places%d" % n, offset=4 * S * (n - 2)))
            nc.vector.memset(places[n][:], 0.0)

        hid = [sb.tile([P, J], F32, name="hid%d" % t) for t in range(4)]
        for t in range(4):
            for h in range(2):
                if t >= 2:
                    acc[t, h] = bank(2 * (t - 2) + h)
                    first_product(t, 0, h)
                first_product(t, 1, h)
                nc.scalar.activation(hid[t][:, BANK * h : BANK * (h + 1)], acc[t, h][:], ACT.Relu)

        picked = sb.tile([P, 4 * I], F32)
        grouped = sb.tile([P, 4 * I], BF16, align_bytes=64)
        h_codes = sb.tile([P, I], U32, align_bytes=64)
        h_plane = sb.tile([P, I], U8, align_bytes=64)

        def gather_hid(t, first, count):
            nc.vector.tensor_copy(
                picked[:, I * t + first : I * t + first + count], hid[t][:].indirect(entries(idx2, first, count))
            )

        def interleave(first, count):
            nc.scalar.copy(
                grouped[:, 4 * first : 4 * (first + count)].rearrange("p (i t) -> p i t", t=4),
                picked[:].rearrange("p (t i) -> p i t", t=4)[:, first : first + count, :],
            )

        def quantise(first, count):
            nc.vector.quantize_mx(
                out=h_codes[:, first : first + count].bitcast(FP8X4),
                scales=h_plane[:, first : first + count],
                in_=grouped[:, 4 * first : 4 * (first + count)],
            )

        def second_product(dst, n, first, count):
            nc.tensor.matmul_mx(
                out=dst,
                lhsT=wb_codes[:, P * n : P * (n + 1)].bitcast(FP8X4),
                lhsT_scale=wb_plane[:, P * n : P * (n + 1)],
                rhs=h_codes[:, first : first + count].bitcast(FP8X4),
                rhs_scale=h_plane[:, first : first + count],
                start=True,
                stop=True,
            )

        def scatter(n, first, count, src):
            nc.vector.tensor_copy(places[n][:].indirect(entries(idx3, first, count)), src)

        for t in range(3):
            gather_hid(t, 0, I)
        gather_hid(3, *CHUNK_A)
        interleave(*CHUNK_A)
        gather_hid(3, CHUNK_B[0], I - CHUNK_B[0])
        quantise(*CHUNK_A)
        interleave(*CHUNK_B)
        bank_a = bank(4)
        for n in range(2):
            second_product(bank_a[:, P * n : P * (n + 1)], n, *CHUNK_A)
        quantise(*CHUNK_B)
        p_a = sb.tile([P, 2 * P], F32)
        nc.vector.tensor_scalar_mul(p_a[:], bank_a[:, 0 : 2 * P], 1.0 / OLD_WEIGHT)
        interleave(*CHUNK_C)
        bank_b = bank(5)
        for n in range(2):
            second_product(bank_b[:, P * n : P * (n + 1)], n, *CHUNK_B)
        p_b = sb.tile([P, 2 * P], F32)
        nc.scalar.activation(p_b[:], bank_b[:, 0 : 2 * P], ACT.Copy, scale=1.0 / OLD_WEIGHT)
        for n in range(2):
            scatter(n, *CHUNK_A, p_a[:, P * n : P * (n + 1)])
        quantise(*CHUNK_C)
        for n in range(2):
            scatter(n, *CHUNK_B, p_b[:, P * n : P * (n + 1)])
        p_c = []
        for n in range(2):
            bank_c = bank(6 + n)
            second_product(bank_c[:, 0 : 2 * P], n, *CHUNK_C)
            p_c.append(sb.tile([P, 2 * P], F32, name="p_c%d" % n, tag="p_c%d" % n))
            nc.scalar.activation(p_c[n][:], bank_c[:, 0 : 2 * P], ACT.Copy, scale=1.0 / OLD_WEIGHT)
        p_whole = {}
        for n in (2, 3):
            bank_whole = bank(2 + n)
            second_product(bank_whole[:], n, 0, I)
            p_whole[n] = sb.tile([P, I], F32, name="p_whole%d" % n)
            nc.scalar.activation(p_whole[n][:], bank_whole[:], ACT.Copy, scale=1.0)

        sum_banks = {0: (2, 3), 1: (0, 1), 2: (1,)}
        back_banks = {0: (6, 7), 1: (2, 3), 2: (4,)}
        sums = {}

        def turn(dst, src, start, stop):
            nc.tensor.matmul(dst, src, ident[:], start=start, stop=stop, is_transpose=True)

        def open_sum(n, addend):
            sums[n] = [bank(b) for b in sum_banks[n]]
            for h in range(len(sums[n])):
                for b in range(4):
                    cols = slice(BANK * h + P * b, BANK * h + P * (b + 1))
                    turn(sums[n][h][:, P * b : P * (b + 1)], addend[:, cols], b == 0, False)

        def close_sum(n, factor):
            halves = range(len(sums[n]))
            for h in halves:
                for b in range(4):
                    cols = slice(BANK * h + P * b, BANK * h + P * (b + 1))
                    turn(sums[n][h][:, P * b : P * (b + 1)], places[n][:, cols], False, b == 3)
            turned = []
            for h in halves:
                turned.append(sb.tile([P, BANK], F32, name="turned%d%d" % (n, h), tag="turned%d%d" % (n, h)))
                nc.scalar.copy(turned[h][:], sums[n][h][:])
            for h in halves:
                back = bank(back_banks[n][h])
                for b in range(4):
                    turn(back[:, P * b : P * (b + 1)], turned[h][:, P * b : P * (b + 1)], True, True)
                result = sb.tile([P, BANK], F32, name="result%d%d" % (n, h))
                nc.scalar.activation(result[:], back[:], ACT.Copy, scale=factor)
                queue = nc.sync if 2 * n + h < 3 else nc.scalar
                queue.dma_start(out[P * n : P * (n + 1), BANK * h : BANK * (h + 1)], result[:])

        open_sum(1, old_pair[0][:, 1, :])
        open_sum(0, old_pair[0][:, 0, :])
        scatter(0, *CHUNK_C, p_c[0][:])
        old_scaled = sb.tile([P, BANK], F32, tag="p_c0")
        nc.scalar.activation(old_scaled[:], old_pair[1][:, 0, 0:BANK], ACT.Copy, scale=OLD_WEIGHT)
        close_sum(0, OLD_WEIGHT)
        scatter(1, *CHUNK_C, p_c[1][:])
        close_sum(1, OLD_WEIGHT)
        open_sum(2, old_scaled[:])
        scatter(2, 0, I, p_whole[2][:])
        close_sum(2, 1.0)
        scatter(3, 0, I, p_whole[3][:])

        tail = sb.tile([P, 3 * BANK], F32, tag="turned11")
        done = 0
        for n, first, count in TAIL:
            cols = slice(first, first + count)
            result = tail[:, done : done + count]
            nc.vector.scalar_tensor_tensor(
                result, old_pair[1][:, n - 2, cols], OLD_WEIGHT, places[n][:, cols], ALU.mult, ALU.add
            )
            nc.sync.dma_start(out[P * n : P * (n + 1), cols], result)
            done = done + count
